import numpy as np
import ml_dtypes


def mxq(x, axis, fmt="e4m3"):
    dtype, down = {"e4m3": (ml_dtypes.float8_e4m3fn, 7), "e5m2": (ml_dtypes.float8_e5m2, 14)}[fmt]
    v = np.moveaxis(np.asarray(x, np.float32).astype(ml_dtypes.bfloat16).astype(np.float64), axis, -1)
    blocks = v.reshape(v.shape[:-1] + (-1, 32))
    amax = np.abs(blocks).max(-1, keepdims=True)
    byte = np.maximum(np.where(amax > 0, np.frexp(amax)[1] - 1 + 127, 0) - down, 1)
    scale = np.exp2(byte - 127.0)
    codes = (blocks / scale).astype(np.float32).astype(dtype).astype(np.float64)
    return np.moveaxis((codes * scale).reshape(v.shape), -1, axis)


WIDE = False


def mx_kscale(k):
    if not WIDE:
        return np.ones(k)
    levels = np.array([10, -10, 5, -5, 0])
    if k % 512:
        return np.exp2(np.random.permutation(np.resize(levels, k // 32))).repeat(32)
    a = np.empty((k // 512, 16))
    for p in range(k // 512):
        a[p, :8] = np.random.permutation(np.resize(levels, 8))
        for g in range(8):
            far = levels[np.abs(levels - a[p, g]) >= 10]
            a[p, g + 8] = far[np.random.randint(len(far))]
    return np.exp2(a.ravel()).repeat(32)


def f64(x):
    return np.asarray(x).astype(np.float64)


def striped(idx):
    return np.tile(idx.reshape(-1, 16).T, (8, 1)).astype(np.uint16)


def unstriped(offs):
    return offs[:16].T.reshape(-1).astype(np.int64)


def striped8(idx):
    return np.concatenate([x.reshape(-1, 16).T for x in idx]).astype(np.uint16)


def runs(offs, k):
    lists = np.stack([offs[16 * r : 16 * r + 16].T.reshape(-1) for r in range(8)]).astype(np.int64)
    return lists[np.arange(k) % 512 // 64]


def pack_weight(w):
    k, n = w.shape
    w = f64(np.asarray(w, np.float32).astype(ml_dtypes.bfloat16)).reshape(k // 32, 32, n)
    amax = np.abs(w).max(1)
    byte = np.clip(np.where(amax > 0, np.frexp(amax)[1] - 1 + 127 - 7, 1), 1, 254)
    scaled = (w * np.exp2(127.0 - byte)[:, None, :]).reshape(k, n).astype(np.float32)
    words = np.ascontiguousarray(scaled.reshape(k // 512, 128, 4, n).transpose(0, 1, 3, 2)).astype(ml_dtypes.float8_e4m3fn).view(np.uint8)
    return words, np.ascontiguousarray(byte.astype(np.uint8).reshape(k // 512, 16, n))


def unpack_weight(words, scales):
    g, p, n, _ = words.shape
    vals = np.ascontiguousarray(words).view(ml_dtypes.float8_e4m3fn).astype(np.float64) * np.repeat(np.exp2(scales.astype(np.float64) - 127.0), 8, axis=1)[..., None]
    return vals.transpose(0, 1, 3, 2).reshape(g * 512, n)

def planes(y):
    n, m = y.shape
    v = y.astype(np.float32).astype(ml_dtypes.bfloat16).astype(np.float64).reshape(n // 32, 32, m)
    top = np.abs(v).max(1)
    byte = np.clip(np.where(top > 0, np.frexp(top)[1] - 1 + 127 - 7, 1), 1, 254)
    codes = (v * np.exp2(127.0 - byte)[:, None, :]).reshape(n, m).astype(np.float32).astype(ml_dtypes.float8_e4m3fn).view(np.uint8)
    words = codes.reshape(n // 512, 128, 4, m).transpose(0, 1, 3, 2)
    return np.ascontiguousarray(words), np.ascontiguousarray(byte.astype(np.uint8).reshape(n // 512, 16, m))


K, T, S, N, H, G, W = 512, 1024, 512, 512, 512, 2048, 1024


def setup_inputs():
    n = np.random.standard_normal
    s = mx_kscale(K)[:, None]
    u = mx_kscale(S)
    packed_xT = pack_weight(n((K, T)) * s)
    packed_w1 = pack_weight(n((K, H)) / np.sqrt(K) / s)
    packed_dT = pack_weight(n((K, G)) / s)
    packed_w2 = pack_weight(n((H, N)) / np.sqrt(2 * H) / u[:, None])
    packed_w3 = pack_weight(n((H, N)) / np.sqrt(2 * H) / u[:, None])
    return {
        "x_words": packed_xT[0],
        "x_scales": packed_xT[1],
        "w1_words": packed_w1[0],
        "w1_scales": packed_w1[1],
        "d_words": packed_dT[0],
        "d_scales": packed_dT[1],
        "gn": (np.random.uniform(0.5, 1.5, (H, 1)) * u[:, None]).astype(np.float32),
        "gk": (np.random.uniform(0.5, 1.5, (H, 1)) * u[:, None]).astype(np.float32),
        "w2_words": packed_w2[0],
        "w2_scales": packed_w2[1],
        "w3_words": packed_w3[0],
        "w3_scales": packed_w3[1],
        "offs": striped(np.random.permutation(T)[:S]),
        "kidx": striped8(np.random.randint(0, G, (8, H))),
        "two": striped(np.random.permutation(T)[:S]),
        "n1": striped(np.random.randint(0, S, W)),
        "n2": striped(np.random.permutation(S)),
        "n3": striped(np.random.permutation(S)),
        "n4": striped(np.random.permutation(S)),
        "n5": striped(np.random.randint(0, S, G)),
    }


def reference(x_words, x_scales, w1_words, w1_scales, d_words, d_scales, gn, gk, w2_words, w2_scales, w3_words, w3_scales, offs, kidx, two, n1, n2, n3, n4, n5):
    xq = unpack_weight(x_words, x_scales)[:, unstriped(offs)]
    y = unpack_weight(w1_words, w1_scales).T @ xq
    mb = y[:, unstriped(n1)]
    mx = mb.reshape(H, S, 2).max(axis=2)
    st = y - mx
    z = f64(gn) * (np.maximum(st, st[:, unstriped(n2)]))
    d_kidx = unpack_weight(d_words, d_scales)[np.arange(K)[:, None], runs(kidx, K)]
    x_two = unpack_weight(x_words, x_scales)[:, unstriped(two)]
    s = 0.0625 * (d_kidx.T @ x_two)
    st2 = s - s[:, unstriped(n3)]
    z2 = f64(gk) * (st2 / (np.abs(st2[:, unstriped(n4)]) + 0.5))
    h = unpack_weight(w2_words, w2_scales).T @ mxq(z, 0, "e4m3") + unpack_weight(w3_words, w3_scales).T @ mxq(z2, 0, "e4m3")
    ex = np.exp(h)
    mb2 = ex[:, unstriped(n5)]
    ms = mb2.reshape(N, S, 4).sum(axis=2)
    out_0 = np.log(ms + ex) - h
    return (out_0,) + planes(out_0)

@@ -1,0 +1,299 @@
+from contextlib import ExitStack
+
+import concourse.mybir as mybir
+
+F32 = mybir.dt.float32
+BF16 = mybir.dt.bfloat16
+I32 = mybir.dt.int32
+U32 = mybir.dt.uint32
+U16 = mybir.dt.uint16
+U8 = mybir.dt.uint8
+FP8X4 = mybir.dt.float8_e4m3fn_x4
+ALU = mybir.AluOpType
+ACT = mybir.ActivationFunctionType
+
+P = 128
+PACK = 4
+S = 512
+T = 1024
+G = 2048
+SPARE = 16
+WIN = S + SPARE
+WIDE = 704
+HALF = S // 2
+CHUNK = 128
+
+FLOPS = 4 * 2 * 512 * 512 * 512
+
+
+def tile_picked_jkeyghopmhopnglse_none_po_kernel(
+    tc, x_words, x_scales, w1_words, w1_scales, d_words, d_scales, gn, gk,
+    w2_words, w2_scales, w3_words, w3_scales, offs, kidx, two, n1, n2, n3, n4, n5,
+    out_0, out_1, out_2,
+):
+    nc = tc.nc
+    with ExitStack() as ctx:
+        lists = ctx.enter_context(tc.tile_pool(name="lists", bufs=1))
+        sb = ctx.enter_context(tc.tile_pool(name="sb", bufs=1))
+        ps = ctx.enter_context(tc.psum_pool(name="ps", bufs=1))
+
+        def tile(name, shape, dtype, tag="", bufs=1):
+            return sb.tile(shape, dtype, name=name, tag=tag or name, bufs=bufs, align_bytes=64)
+
+        def load_list(name, src):
+            held = lists.tile(list(src.shape), U16, name=name)
+            nc.sync.dma_start(held[:], src)
+            return held
+
+        def load_words(name, src):
+            held = tile(name, [P, src.shape[2]], I32)
+            nc.sync.dma_start(held[:], src[0].rearrange("p n t -> p (n t)").bitcast(I32))
+            return held
+
+        def load_scale_rows(plane, first, src):
+            for q in range(4):
+                nc.sync.dma_start(
+                    plane[32 * q + first : 32 * q + first + 4, :].bitcast(I32),
+                    src[0, 4 * q : 4 * q + 4, :].bitcast(I32),
+                )
+
+        def deal_words(name, src):
+            dealt = tile(name, [P, S], I32)
+            nc.vector.tensor_copy(
+                dealt[:].rearrange("p (t c i) -> p c t i", t=PACK, i=4),
+                src.rearrange("p (c i t) -> p c t i", t=PACK, i=4),
+            )
+            return dealt
+
+        def deal_bytes(name, src):
+            dealt = tile(name, [P, S], U8)
+            nc.vector.tensor_copy(
+                dealt[:].rearrange("p (t m) -> p t m", t=PACK),
+                src.rearrange("p (m t) -> p t m", t=PACK),
+            )
+            return dealt
+
+        def pick(name, table, offsets, dtype):
+            picked = tile(name, [P, S], dtype)
+            nc.vector.tensor_copy(picked[:], table.indirect(offsets[:]))
+            return picked
+
+        def gather(engine, out, window, offsets):
+            if engine == "v":
+                nc.vector.tensor_copy(out, window[:].indirect(offsets))
+            else:
+                nc.scalar.activation(out, window[:].indirect(offsets), ACT.Copy)
+
+        def window(name, width=WIN):
+            held = tile(name, [P, width], F32)
+            nc.gpsimd.memset(held[:, S:], 0.0)
+            return held
+
+        def product(bank, cols, words, plane, t, moving_words, moving_plane, start, stop):
+            rows = slice(P * t, P * (t + 1))
+            nc.tensor.matmul_mx(
+                out=bank,
+                lhsT=words[:, rows].bitcast(FP8X4),
+                lhsT_scale=plane[:, rows],
+                rhs=moving_words[:, cols].bitcast(FP8X4),
+                rhs_scale=moving_plane[:, cols],
+                start=start,
+                stop=stop,
+            )
+
+        def woven(ap):
+            return ap.rearrange("p (c i) t -> p c t i", i=2)
+
+        def planes(ap):
+            return ap.rearrange("p t (c i) -> p c t i", i=2)
+
+        ds = tile("ds", [P, G], U8)
+        nc.vector.memset(ds[:].bitcast(I32), 0)
+        xs = tile("xs", [P, T], U8)
+        nc.vector.memset(xs[:].bitcast(I32), 0)
+        w1s = tile("w1s", [P, S], U8)
+        nc.gpsimd.memset(w1s[:].bitcast(I32), 0)
+        key_plane = tile("key_plane", [P, S], U8)
+        nc.gpsimd.memset(key_plane[:].bitcast(I32), 0)
+        consts = tile("consts", [P, 2], F32)
+        nc.gpsimd.memset(consts[:, 0:1], 8.0)
+        nc.gpsimd.memset(consts[:, 1:2], 1.0)
+
+        kidx_t = load_list("kidx_t", kidx)
+        nc.sync.dma_start(ds[0:P:8, :].bitcast(I32), d_scales[0].bitcast(I32))
+        offs_t = load_list("offs_t", offs)
+        xw = load_words("xw", x_words)
+        load_scale_rows(xs, 0, x_scales)
+        w1w = load_words("w1w", w1_words)
+        load_scale_rows(w1s, 0, w1_scales)
+        two_t = load_list("two_t", two)
+        dw = load_words("dw", d_words)
+        n1_t = load_list("n1_t", n1)
+
+        ks = pick("ks", ds[:], kidx_t, U8)
+        ksd = deal_bytes("ksd", ks[:])
+        for q in range(4):
+            nc.sync.dma_start(
+                key_plane[32 * q : 32 * q + 4, :].bitcast(I32),
+                ksd[32 * q : 32 * q + 32 : 8, :].bitcast(I32),
+            )
+
+        gk_t = tile("gk_t", [P, PACK], F32)
+        nc.sync.dma_start(gk_t[:], gk.rearrange("(p t) o -> p (t o)", t=PACK))
+        n3_t = load_list("n3_t", n3)
+        n2_t = load_list("n2_t", n2)
+        n4_t = load_list("n4_t", n4)
+        gn_t = tile("gn_t", [P, PACK], F32)
+        nc.sync.dma_start(gn_t[:], gn.rearrange("(p t) o -> p (t o)", t=PACK))
+        n5_t = load_list("n5_t", n5)
+        w3w = load_words("w3w", w3_words)
+        w2w = load_words("w2w", w2_words)
+
+        x1w = pick("x1w", xw[:].bitcast(U32), offs_t, U32)
+        x1s = pick("x1s", xs[:], offs_t, U8)
+        w1d = deal_words("w1d", w1w[:])
+        w1p = deal_bytes("w1p", w1s[:])
+        everything = slice(0, S)
+        y_ps = [ps.tile([P, S], F32, name="y%d" % t, tag="bank%d" % t) for t in range(PACK)]
+        for t in range(PACK):
+            product(y_ps[t][:], everything, w1d, w1p, t, x1w, x1s, True, True)
+
+        big = [tile("big%d" % t, [P, 4 * S], F32) for t in range(PACK)]
+        y = [window("yw%d" % t) for t in range(PACK)]
+
+        def members(engine, t):
+            for u in range(2):
+                gather(engine, big[t][:, (2 + u) * S : (3 + u) * S], y[t], n1_t[:, 32 * u : 32 * (u + 1)])
+
+        for t in range(2):
+            nc.scalar.activation(y[t][:, :S], y_ps[t][:], ACT.Copy)
+            members("s", t)
+
+        x2w = pick("x2w", xw[:].bitcast(U32), two_t, U32)
+        x2s = pick("x2s", xs[:], two_t, U8)
+        kw = pick("kw", dw[:].bitcast(U32), kidx_t, U32)
+        kwd = deal_words("kwd", kw[:].bitcast(I32))
+        s_ps = [ps.tile([P, S], F32, name="s%d" % t, tag="bank%d" % (PACK + t)) for t in range(PACK)]
+        for t in range(PACK):
+            product(s_ps[t][:], everything, kwd, key_plane, t, x2w, x2s, True, True)
+
+        w23s = tile("w23s", [P, S], U8, tag="ksd")
+        nc.gpsimd.memset(w23s[:].bitcast(I32), 0)
+        load_scale_rows(w23s, 0, w2_scales)
+        load_scale_rows(w23s, 4, w3_scales)
+
+        gk_safe = tile("gk_safe", [P, PACK], F32)
+        nc.vector.scalar_tensor_tensor(gk_safe[:], gk_t[:], 0.0, gk_t[:], ALU.is_equal, ALU.add)
+        gk_inv = tile("gk_inv", [P, PACK], F32)
+        nc.vector.reciprocal(gk_inv[:], gk_safe[:])
+
+        sg = [window("sg%d" % t, WIN if t % 2 else WIDE) for t in range(PACK)]
+        diff = tile("diff", [P, PACK, S], F32)
+        size = tile("size", [P, PACK, S], F32, tag="size")
+        for t in range(PACK):
+            nc.scalar.activation(sg[t][:, :S], s_ps[t][:], ACT.Copy, scale=gk_t[:, t : t + 1])
+            gather("s" if t % 2 else "v", big[t][:, S : 2 * S], sg[t], n3_t[:])
+            nc.vector.scalar_tensor_tensor(
+                diff[:, t, :], s_ps[t][:], gk_t[:, t : t + 1], big[t][:, S : 2 * S], ALU.mult, ALU.subtract
+            )
+        for t in range(2, PACK):
+            nc.vector.tensor_copy(y[t][:, :S], y_ps[t][:])
+        members("s", 3)
+        members("v", 2)
+        for t in range(PACK):
+            nc.scalar.activation(size[:, t, :], diff[:, t, :], ACT.Abs, scale=gk_inv[:, t : t + 1])
+        for t in range(PACK):
+            nc.scalar.activation(big[t][:, :S], size[:, t, :], ACT.Ln, bias=consts[:, 0:1])
+
+        larger = tile("larger", [P, PACK, S], F32)
+        st = [window("st%d" % t, WIN if t == 0 else WIDE) for t in range(PACK)]
+        other = tile("other", [P, PACK, S], F32)
+        best = tile("best", [P, PACK, S], F32)
+        for t in range(PACK):
+            pairs = big[t][:, 2 * S :].rearrange("p (j u) -> p j u", u=2)
+            nc.vector.tensor_tensor(larger[:, t, :], pairs[:, :, 0], pairs[:, :, 1], ALU.max)
+            nc.vector.tensor_tensor(st[t][:, :S], y[t][:, :S], larger[:, t, :], ALU.subtract)
+            gather("s" if t == 0 else "v", other[:, t, :], st[t], n2_t[:])
+            nc.vector.tensor_tensor(best[:, t, :], st[t][:, :S], other[:, t, :], ALU.max)
+
+        inv = tile("inv", [P, PACK, S], F32, tag="size")
+        for t in range(PACK):
+            nc.scalar.activation(inv[:, t, :], big[t][:].indirect(n4_t[:]), ACT.Exp, scale=-1.0)
+
+        w2d = deal_words("w2d", w2w[:])
+        w3d = deal_words("w3d", w3w[:])
+        w23p = deal_bytes("w23p", w23s[:])
+
+        halves = [slice(HALF * u, HALF * (u + 1)) for u in range(2)]
+        h_ps = [
+            [ps.tile([P, HALF], F32, name="h%d%d" % (u, t), tag="bank%d" % (PACK * u + t)) for t in range(PACK)]
+            for u in range(2)
+        ]
+        zb = tile("zb", [P, S, PACK], BF16)
+        zw = tile("zw", [P, S], U32)
+        zs = tile("zs", [P, S], U8)
+        gains = gn_t[:].unsqueeze(1).unsqueeze(3).to_broadcast([P, S // 2, PACK, 2])
+        nc.vector.tensor_tensor(woven(zb[:]), planes(best[:]), gains, ALU.mult)
+        nc.vector.quantize_mx(out=zw[:].bitcast(FP8X4), scales=zs[:], in_=zb[:].rearrange("p j t -> p (j t)"))
+        for u in range(2):
+            for t in range(PACK):
+                product(h_ps[u][t][:], halves[u], w2d, w23p, t, zw, zs, True, False)
+
+        z2w = tile("z2w", [P, S], U32)
+        z2s = tile("z2s", [P, S], U8)
+        ex = [window("ex%d" % t) for t in range(PACK)]
+        ex_inv = [tile("ex_inv%d" % u, [P, PACK, HALF], F32) for u in range(2)]
+
+        def inverse(u):
+            for t in range(PACK):
+                nc.scalar.activation(ex_inv[u][:, t, :], h_ps[u][t][:], ACT.Exp, scale=-1.0)
+
+        for u in range(2):
+            z2b = tile("z2b%d" % u, [P, HALF, PACK], BF16, tag="z2b")
+            nc.vector.tensor_tensor(
+                woven(z2b[:]), planes(diff[:, :, halves[u]]), planes(inv[:, :, halves[u]]), ALU.mult
+            )
+            nc.vector.quantize_mx(
+                out=z2w[:, halves[u]].bitcast(FP8X4),
+                scales=z2s[:, halves[u]],
+                in_=z2b[:].rearrange("p j t -> p (j t)"),
+            )
+            for t in range(PACK):
+                product(h_ps[u][t][:], halves[u], w3d, w23p[4:P, :], t, z2w, z2s, False, True)
+            for t in range(PACK):
+                nc.scalar.activation(ex[t][:, halves[u]], h_ps[u][t][:], ACT.Exp)
+
+        ow = tile("ow", [P, S], U32)
+        osc = tile("osc", [P, S], U8)
+        out_rows = out_0.rearrange("(p t) j -> p t j", t=PACK)
+        out_words = out_1[0].rearrange("p n t -> p (n t)").bitcast(I32)
+        chunks = [slice(CHUNK * c, CHUNK * (c + 1)) for c in range(S // CHUNK)]
+        ratio = tile("ratio", [P, len(chunks), PACK, CHUNK], F32)
+        for c, cols in enumerate(chunks):
+            fetched = tile("fetched%d" % c, [P, PACK, CHUNK * 4], F32)
+            on_vector = 2 if c in (0, 3) else 1
+            for t in range(PACK):
+                gather("v" if t < on_vector else "s", fetched[:, t, :], ex[t], n5_t[:, 32 * c : 32 * (c + 1)])
+            if c < 2:
+                inverse(c)
+            quads = fetched[:].rearrange("p t (j u) -> p (t j) u", u=4)
+            twos = tile("twos%d" % c, [P, PACK * CHUNK, 2], F32, tag="twos")
+            nc.vector.tensor_tensor(twos[:], quads[:, :, 0:2], quads[:, :, 2:4], ALU.add)
+            total = tile("total%d" % c, [P, PACK, CHUNK], F32, tag="total", bufs=2)
+            nc.vector.tensor_tensor(total[:].rearrange("p t j -> p (t j)"), twos[:, :, 0], twos[:, :, 1], ALU.add)
+            nc.vector.tensor_tensor(ratio[:, c, :, :], total[:], ex_inv[c // 2][:, :, chunks[c % 2]], ALU.mult)
+        for c, cols in enumerate(chunks):
+            result = tile("result%d" % c, [P, PACK, CHUNK], F32)
+            nc.scalar.activation(result[:], ratio[:, c, :, :], ACT.Ln, bias=consts[:, 1:2])
+            nc.sync.dma_start(out_rows[:, :, cols], result[:])
+            rounded = tile("rounded%d" % c, [P, CHUNK, PACK], BF16)
+            nc.vector.tensor_copy(woven(rounded[:]), planes(result[:]))
+            nc.vector.quantize_mx(
+                out=ow[:, cols].bitcast(FP8X4), scales=osc[:, cols], in_=rounded[:].rearrange("p j t -> p (j t)")
+            )
+            if c % 2:
+                nc.sync.dma_start(out_words[:, halves[c // 2]], ow[:, halves[c // 2]].bitcast(I32))
+        for q in range(4):
+            (nc.sync if q < 2 else nc.scalar).dma_start(
+                out_2[0, 4 * q : 4 * q + 4, :].bitcast(I32), osc[32 * q : 32 * q + 4, :].bitcast(I32)
+            )

@@ -1,6 +1,7 @@
 from contextlib import ExitStack
 
 import concourse.mybir as mybir
+from concourse.masks import make_identity
 
 F32 = mybir.dt.float32
 BF16 = mybir.dt.bfloat16
@@ -22,6 +23,8 @@ WIN = S + SPARE
 WIDE = 704
 HALF = S // 2
 CHUNK = 128
+ON_VECTOR = (2, 2, 2, 2)
+ORDER = (0, 2, 1, 3)
 
 FLOPS = 4 * 2 * 512 * 512 * 512
 
@@ -45,14 +48,14 @@ def tile_picked_jkeyghopmhopnglse_none_po_kernel(
             nc.sync.dma_start(held[:], src)
             return held
 
-        def load_words(name, src):
-            held = tile(name, [P, src.shape[2]], I32)
-            nc.sync.dma_start(held[:], src[0].rearrange("p n t -> p (n t)").bitcast(I32))
+        def load_words(queue, name, src, tag=""):
+            held = tile(name, [P, src.shape[2]], I32, tag=tag)
+            queue.dma_start(held[:], src[0].rearrange("p n t -> p (n t)").bitcast(I32))
             return held
 
-        def load_scale_rows(plane, first, src):
+        def load_scale_rows(queue, plane, first, src):
             for q in range(4):
-                nc.sync.dma_start(
+                queue.dma_start(
                     plane[32 * q + first : 32 * q + first + 4, :].bitcast(I32),
                     src[0, 4 * q : 4 * q + 4, :].bitcast(I32),
                 )
@@ -73,8 +76,8 @@ def tile_picked_jkeyghopmhopnglse_none_po_kernel(
             )
             return dealt
 
-        def pick(name, table, offsets, dtype):
-            picked = tile(name, [P, S], dtype)
+        def pick(name, table, offsets, dtype, tag=""):
+            picked = tile(name, [P, S], dtype, tag=tag)
             nc.vector.tensor_copy(picked[:], table.indirect(offsets[:]))
             return picked
 
@@ -107,37 +110,31 @@ def tile_picked_jkeyghopmhopnglse_none_po_kernel(
         def planes(ap):
             return ap.rearrange("p t (c i) -> p c t i", i=2)
 
+        xs = tile("xs", [P, T], U8)
+        nc.gpsimd.memset(xs[:].bitcast(I32), 0)
+        w1s = tile("w1s", [P, S], U8)
+        nc.vector.memset(w1s[:].bitcast(I32), 0)
         ds = tile("ds", [P, G], U8)
         nc.vector.memset(ds[:].bitcast(I32), 0)
-        xs = tile("xs", [P, T], U8)
-        nc.vector.memset(xs[:].bitcast(I32), 0)
-        w1s = tile("w1s", [P, S], U8)
-        nc.gpsimd.memset(w1s[:].bitcast(I32), 0)
         key_plane = tile("key_plane", [P, S], U8)
         nc.gpsimd.memset(key_plane[:].bitcast(I32), 0)
         consts = tile("consts", [P, 2], F32)
         nc.gpsimd.memset(consts[:, 0:1], 8.0)
         nc.gpsimd.memset(consts[:, 1:2], 1.0)
 
+        ident = tile("ident", [P, P], F32)
+        make_identity(nc, ident[:])
+
+        offs_t = load_list("offs_t", offs)
+        xw = load_words(nc.sync, "xw", x_words)
+        load_scale_rows(nc.sync, xs, 0, x_scales)
+        w1w = load_words(nc.sync, "w1w", w1_words)
+        load_scale_rows(nc.sync, w1s, 0, w1_scales)
         kidx_t = load_list("kidx_t", kidx)
         nc.sync.dma_start(ds[0:P:8, :].bitcast(I32), d_scales[0].bitcast(I32))
-        offs_t = load_list("offs_t", offs)
-        xw = load_words("xw", x_words)
-        load_scale_rows(xs, 0, x_scales)
-        w1w = load_words("w1w", w1_words)
-        load_scale_rows(w1s, 0, w1_scales)
-        two_t = load_list("two_t", two)
-        dw = load_words("dw", d_words)
         n1_t = load_list("n1_t", n1)
-
-        ks = pick("ks", ds[:], kidx_t, U8)
-        ksd = deal_bytes("ksd", ks[:])
-        for q in range(4):
-            nc.sync.dma_start(
-                key_plane[32 * q : 32 * q + 4, :].bitcast(I32),
-                ksd[32 * q : 32 * q + 32 : 8, :].bitcast(I32),
-            )
-
+        two_t = load_list("two_t", two)
+        dw = load_words(nc.sync, "dw", d_words)
         gk_t = tile("gk_t", [P, PACK], F32)
         nc.sync.dma_start(gk_t[:], gk.rearrange("(p t) o -> p (t o)", t=PACK))
         n3_t = load_list("n3_t", n3)
@@ -146,16 +143,14 @@ def tile_picked_jkeyghopmhopnglse_none_po_kernel(
         gn_t = tile("gn_t", [P, PACK], F32)
         nc.sync.dma_start(gn_t[:], gn.rearrange("(p t) o -> p (t o)", t=PACK))
         n5_t = load_list("n5_t", n5)
-        w3w = load_words("w3w", w3_words)
-        w2w = load_words("w2w", w2_words)
 
         x1w = pick("x1w", xw[:].bitcast(U32), offs_t, U32)
         x1s = pick("x1s", xs[:], offs_t, U8)
         w1d = deal_words("w1d", w1w[:])
         w1p = deal_bytes("w1p", w1s[:])
         everything = slice(0, S)
-        y_ps = [ps.tile([P, S], F32, name="y%d" % t, tag="bank%d" % t) for t in range(PACK)]
-        for t in range(PACK):
+        y_ps = [ps.tile([P, S], F32, name="y%d" % t, tag="bank%d" % t) for t in range(2)]
+        for t in range(2):
             product(y_ps[t][:], everything, w1d, w1p, t, x1w, x1s, True, True)
 
         big = [tile("big%d" % t, [P, 4 * S], F32) for t in range(PACK)]
@@ -169,7 +164,14 @@ def tile_picked_jkeyghopmhopnglse_none_po_kernel(
             nc.scalar.activation(y[t][:, :S], y_ps[t][:], ACT.Copy)
             members("s", t)
 
-        x2w = pick("x2w", xw[:].bitcast(U32), two_t, U32)
+        ks = pick("ks", ds[:], kidx_t, U8)
+        ksd = deal_bytes("ksd", ks[:])
+        for q in range(4):
+            nc.sync.dma_start(
+                key_plane[32 * q : 32 * q + 4, :].bitcast(I32),
+                ksd[32 * q : 32 * q + 32 : 8, :].bitcast(I32),
+            )
+        x2w = pick("x2w", xw[:].bitcast(U32), two_t, U32, tag="ks")
         x2s = pick("x2s", xs[:], two_t, U8)
         kw = pick("kw", dw[:].bitcast(U32), kidx_t, U32)
         kwd = deal_words("kwd", kw[:].bitcast(I32))
@@ -177,27 +179,31 @@ def tile_picked_jkeyghopmhopnglse_none_po_kernel(
         for t in range(PACK):
             product(s_ps[t][:], everything, kwd, key_plane, t, x2w, x2s, True, True)
 
+        w2w = load_words(nc.sync, "w2w", w2_words, tag="xw")
+        w3w = load_words(nc.sync, "w3w", w3_words, tag="dw")
         w23s = tile("w23s", [P, S], U8, tag="ksd")
         nc.gpsimd.memset(w23s[:].bitcast(I32), 0)
-        load_scale_rows(w23s, 0, w2_scales)
-        load_scale_rows(w23s, 4, w3_scales)
+        load_scale_rows(nc.sync, w23s, 0, w2_scales)
+        load_scale_rows(nc.sync, w23s, 4, w3_scales)
 
         gk_safe = tile("gk_safe", [P, PACK], F32)
         nc.vector.scalar_tensor_tensor(gk_safe[:], gk_t[:], 0.0, gk_t[:], ALU.is_equal, ALU.add)
         gk_inv = tile("gk_inv", [P, PACK], F32)
         nc.vector.reciprocal(gk_inv[:], gk_safe[:])
 
-        sg = [window("sg%d" % t, WIN if t % 2 else WIDE) for t in range(PACK)]
+        sg = [window("sg%d" % t, WIDE if t in (2,) else WIN) for t in range(PACK)]
         diff = tile("diff", [P, PACK, S], F32)
         size = tile("size", [P, PACK, S], F32, tag="size")
         for t in range(PACK):
             nc.scalar.activation(sg[t][:, :S], s_ps[t][:], ACT.Copy, scale=gk_t[:, t : t + 1])
-            gather("s" if t % 2 else "v", big[t][:, S : 2 * S], sg[t], n3_t[:])
+            gather("v" if t in (2,) else "s", big[t][:, S : 2 * S], sg[t], n3_t[:])
             nc.vector.scalar_tensor_tensor(
                 diff[:, t, :], s_ps[t][:], gk_t[:, t : t + 1], big[t][:, S : 2 * S], ALU.mult, ALU.subtract
             )
         for t in range(2, PACK):
-            nc.vector.tensor_copy(y[t][:, :S], y_ps[t][:])
+            late = ps.tile([P, S], F32, name="y%d" % t, tag="bank%d" % (2 + t))
+            product(late[:], everything, w1d, w1p, t, x1w, x1s, True, True)
+            nc.vector.tensor_copy(y[t][:, :S], late[:])
         members("s", 3)
         members("v", 2)
         for t in range(PACK):
@@ -205,16 +211,16 @@ def tile_picked_jkeyghopmhopnglse_none_po_kernel(
         for t in range(PACK):
             nc.scalar.activation(big[t][:, :S], size[:, t, :], ACT.Ln, bias=consts[:, 0:1])
 
-        larger = tile("larger", [P, PACK, S], F32)
+        larger = tile("larger", [P, PACK, S], F32, tag="kw")
         st = [window("st%d" % t, WIN if t == 0 else WIDE) for t in range(PACK)]
-        other = tile("other", [P, PACK, S], F32)
+        other = [tile("other%d" % t, [P, S], F32, tag="sg%d" % (PACK - 1 - t)) for t in range(PACK)]
         best = tile("best", [P, PACK, S], F32)
         for t in range(PACK):
             pairs = big[t][:, 2 * S :].rearrange("p (j u) -> p j u", u=2)
             nc.vector.tensor_tensor(larger[:, t, :], pairs[:, :, 0], pairs[:, :, 1], ALU.max)
             nc.vector.tensor_tensor(st[t][:, :S], y[t][:, :S], larger[:, t, :], ALU.subtract)
-            gather("s" if t == 0 else "v", other[:, t, :], st[t], n2_t[:])
-            nc.vector.tensor_tensor(best[:, t, :], st[t][:, :S], other[:, t, :], ALU.max)
+            gather("s" if t == 0 else "v", other[t][:], st[t], n2_t[:])
+            nc.vector.tensor_tensor(best[:, t, :], st[t][:, :S], other[t][:], ALU.max)
 
         inv = tile("inv", [P, PACK, S], F32, tag="size")
         for t in range(PACK):
@@ -242,14 +248,11 @@ def tile_picked_jkeyghopmhopnglse_none_po_kernel(
         z2w = tile("z2w", [P, S], U32)
         z2s = tile("z2s", [P, S], U8)
         ex = [window("ex%d" % t) for t in range(PACK)]
-        ex_inv = [tile("ex_inv%d" % u, [P, PACK, HALF], F32) for u in range(2)]
-
-        def inverse(u):
-            for t in range(PACK):
-                nc.scalar.activation(ex_inv[u][:, t, :], h_ps[u][t][:], ACT.Exp, scale=-1.0)
+        h_kept = [tile("h_kept%d" % u, [P, PACK, HALF], F32) for u in range(2)]
+        ex_inv = tile("ex_inv", [P, PACK, HALF], F32)
 
         for u in range(2):
-            z2b = tile("z2b%d" % u, [P, HALF, PACK], BF16, tag="z2b")
+            z2b = tile("z2b%d" % u, [P, HALF, PACK], BF16, tag="zb")
             nc.vector.tensor_tensor(
                 woven(z2b[:]), planes(diff[:, :, halves[u]]), planes(inv[:, :, halves[u]]), ALU.mult
             )
@@ -268,26 +271,58 @@ def tile_picked_jkeyghopmhopnglse_none_po_kernel(
         out_rows = out_0.rearrange("(p t) j -> p t j", t=PACK)
         out_words = out_1[0].rearrange("p n t -> p (n t)").bitcast(I32)
         chunks = [slice(CHUNK * c, CHUNK * (c + 1)) for c in range(S // CHUNK)]
-        ratio = tile("ratio", [P, len(chunks), PACK, CHUNK], F32)
-        for c, cols in enumerate(chunks):
-            fetched = tile("fetched%d" % c, [P, PACK, CHUNK * 4], F32)
-            on_vector = 2 if c in (0, 3) else 1
+        for t in range(PACK):
+            nc.vector.tensor_copy(h_kept[0][:, t, :], h_ps[0][t][:])
+        before_log = {}
+        for c in ORDER:
+            cols = chunks[c]
+            fetched = tile("fetched%d" % c, [P, PACK, CHUNK, 4], F32)
             for t in range(PACK):
-                gather("v" if t < on_vector else "s", fetched[:, t, :], ex[t], n5_t[:, 32 * c : 32 * (c + 1)])
+                gather(
+                    "v" if t < ON_VECTOR[c] else "s",
+                    fetched[:, t, :, :].rearrange("p j u -> p (j u)"),
+                    ex[t],
+                    n5_t[:, 32 * c : 32 * (c + 1)],
+                )
+            if c == 0:
+                for t in range(PACK):
+                    nc.scalar.activation(ex_inv[:, t, :], h_ps[1][t][:], ACT.Exp, scale=-1.0)
             if c < 2:
-                inverse(c)
-            quads = fetched[:].rearrange("p t (j u) -> p (t j) u", u=4)
+                turned = ps.tile([P, PACK, CHUNK], F32, name="turned%d" % c, tag="bank%d" % c)
+                for t in range(PACK):
+                    terms = [ex[t][:, cols]] + [fetched[:, t, :, u] for u in range(4)]
+                    for n, term in enumerate(terms):
+                        nc.tensor.matmul(
+                            turned[:, t, :], term, ident[:], is_transpose=True, start=n == 0, stop=n == 4
+                        )
+                before_log[c] = turned
+                continue
+            quads = fetched[:].rearrange("p t j u -> p (t j) u")
             twos = tile("twos%d" % c, [P, PACK * CHUNK, 2], F32, tag="twos")
             nc.vector.tensor_tensor(twos[:], quads[:, :, 0:2], quads[:, :, 2:4], ALU.add)
-            total = tile("total%d" % c, [P, PACK, CHUNK], F32, tag="total", bufs=2)
+            total = tile("total%d" % c, [P, PACK, CHUNK], F32)
             nc.vector.tensor_tensor(total[:].rearrange("p t j -> p (t j)"), twos[:, :, 0], twos[:, :, 1], ALU.add)
-            nc.vector.tensor_tensor(ratio[:, c, :, :], total[:], ex_inv[c // 2][:, :, chunks[c % 2]], ALU.mult)
-        for c, cols in enumerate(chunks):
+            ratio = tile("ratio%d" % c, [P, PACK, CHUNK], F32)
+            nc.vector.tensor_tensor(ratio[:], total[:], ex_inv[:, :, chunks[c - 2]], ALU.mult)
+            before_log[c] = ratio
+        for c in (0, 1, 2, 3):
+            cols = chunks[c]
             result = tile("result%d" % c, [P, PACK, CHUNK], F32)
-            nc.scalar.activation(result[:], ratio[:, c, :, :], ACT.Ln, bias=consts[:, 1:2])
+            if c < 2:
+                logs = tile("logs%d" % c, [P, PACK, CHUNK], F32)
+                nc.scalar.activation(logs[:], before_log[c][:], ACT.Ln)
+                back = ps.tile([P, PACK, CHUNK], F32, name="back%d" % c, tag="bank%d" % (2 + c))
+                for t in range(PACK):
+                    nc.tensor.transpose(back[:, t, :], logs[:, t, :], ident[:])
+                nc.vector.tensor_tensor(result[:], back[:], h_kept[c // 2][:, :, chunks[c % 2]], ALU.subtract)
+            else:
+                nc.scalar.activation(result[:], before_log[c][:], ACT.Ln, bias=consts[:, 1:2])
             nc.sync.dma_start(out_rows[:, :, cols], result[:])
             rounded = tile("rounded%d" % c, [P, CHUNK, PACK], BF16)
-            nc.vector.tensor_copy(woven(rounded[:]), planes(result[:]))
+            if c in (2, 3):
+                nc.scalar.copy(woven(rounded[:]), planes(result[:]))
+            else:
+                nc.vector.tensor_copy(woven(rounded[:]), planes(result[:]))
             nc.vector.quantize_mx(
                 out=ow[:, cols].bitcast(FP8X4), scales=osc[:, cols], in_=rounded[:].rearrange("p j t -> p (j t)")
             )

@@ -23,6 +23,9 @@ WIN = S + SPARE
 WIDE = 704
 HALF = S // 2
 CHUNK = 128
+SIGN_COLUMNS = 64
+EARLY = (3, 2)
+LATE = (1, 0)
 ON_VECTOR = (2, 2, 2, 2)
 ORDER = (0, 2, 1, 3)
 
@@ -125,11 +128,20 @@ def tile_picked_jkeyghopmhopnglse_none_po_kernel(
         ident = tile("ident", [P, P], F32)
         make_identity(nc, ident[:])
 
+        unread = tile("unread", [P, 1], F32)
+        nc.scalar.activation(unread[:], consts[:, 1:2], ACT.Ln)
+
         offs_t = load_list("offs_t", offs)
         xw = load_words(nc.sync, "xw", x_words)
         load_scale_rows(nc.sync, xs, 0, x_scales)
         w1w = load_words(nc.sync, "w1w", w1_words)
         load_scale_rows(nc.sync, w1s, 0, w1_scales)
+        gn_t = tile("gn_t", [P, PACK], F32)
+        nc.sync.dma_start(gn_t[:], gn.rearrange("(p t) o -> p (t o)", t=PACK))
+        gn_size = tile("gn_size", [P, PACK], F32)
+        nc.scalar.activation(gn_size[:], gn_t[:], ACT.Abs)
+        gn_sign = tile("gn_sign", [P, SIGN_COLUMNS, PACK], BF16)
+        nc.scalar.activation(gn_sign[:], gn_t[:].unsqueeze(1).to_broadcast([P, SIGN_COLUMNS, PACK]), ACT.Sign)
         kidx_t = load_list("kidx_t", kidx)
         nc.sync.dma_start(ds[0:P:8, :].bitcast(I32), d_scales[0].bitcast(I32))
         n1_t = load_list("n1_t", n1)
@@ -140,8 +152,6 @@ def tile_picked_jkeyghopmhopnglse_none_po_kernel(
         n3_t = load_list("n3_t", n3)
         n2_t = load_list("n2_t", n2)
         n4_t = load_list("n4_t", n4)
-        gn_t = tile("gn_t", [P, PACK], F32)
-        nc.sync.dma_start(gn_t[:], gn.rearrange("(p t) o -> p (t o)", t=PACK))
         n5_t = load_list("n5_t", n5)
 
         x1w = pick("x1w", xw[:].bitcast(U32), offs_t, U32)
@@ -149,8 +159,8 @@ def tile_picked_jkeyghopmhopnglse_none_po_kernel(
         w1d = deal_words("w1d", w1w[:])
         w1p = deal_bytes("w1p", w1s[:])
         everything = slice(0, S)
-        y_ps = [ps.tile([P, S], F32, name="y%d" % t, tag="bank%d" % t) for t in range(2)]
-        for t in range(2):
+        y_ps = {t: ps.tile([P, S], F32, name="y%d" % t, tag="bank%d" % t) for t in EARLY}
+        for t in EARLY:
             product(y_ps[t][:], everything, w1d, w1p, t, x1w, x1s, True, True)
 
         big = [tile("big%d" % t, [P, 4 * S], F32) for t in range(PACK)]
@@ -160,8 +170,8 @@ def tile_picked_jkeyghopmhopnglse_none_po_kernel(
             for u in range(2):
                 gather(engine, big[t][:, (2 + u) * S : (3 + u) * S], y[t], n1_t[:, 32 * u : 32 * (u + 1)])
 
-        for t in range(2):
-            nc.scalar.activation(y[t][:, :S], y_ps[t][:], ACT.Copy)
+        for t in EARLY:
+            nc.scalar.activation(y[t][:, :S], y_ps[t][:], ACT.Copy, scale=gn_size[:, t : t + 1])
             members("s", t)
 
         ks = pick("ks", ds[:], kidx_t, U8)
@@ -191,36 +201,35 @@ def tile_picked_jkeyghopmhopnglse_none_po_kernel(
         gk_inv = tile("gk_inv", [P, PACK], F32)
         nc.vector.reciprocal(gk_inv[:], gk_safe[:])
 
-        sg = [window("sg%d" % t, WIDE if t in (2,) else WIN) for t in range(PACK)]
+        sg = [window("sg%d" % t, WIDE if t in (3,) else WIN) for t in range(PACK)]
         diff = tile("diff", [P, PACK, S], F32)
         size = tile("size", [P, PACK, S], F32, tag="size")
         for t in range(PACK):
             nc.scalar.activation(sg[t][:, :S], s_ps[t][:], ACT.Copy, scale=gk_t[:, t : t + 1])
-            gather("v" if t in (2,) else "s", big[t][:, S : 2 * S], sg[t], n3_t[:])
+            gather("v" if t in (3,) else "s", big[t][:, S : 2 * S], sg[t], n3_t[:])
             nc.vector.scalar_tensor_tensor(
                 diff[:, t, :], s_ps[t][:], gk_t[:, t : t + 1], big[t][:, S : 2 * S], ALU.mult, ALU.subtract
             )
-        for t in range(2, PACK):
-            late = ps.tile([P, S], F32, name="y%d" % t, tag="bank%d" % (2 + t))
+        for n, t in enumerate(LATE):
+            late = ps.tile([P, S], F32, name="y%d" % t, tag="bank%d" % (PACK + n))
             product(late[:], everything, w1d, w1p, t, x1w, x1s, True, True)
-            nc.vector.tensor_copy(y[t][:, :S], late[:])
-        members("s", 3)
-        members("v", 2)
+            nc.scalar.activation(y[t][:, :S], late[:], ACT.Copy, scale=gn_size[:, t : t + 1])
+        members("s", LATE[1])
+        members("v", LATE[0])
         for t in range(PACK):
             nc.scalar.activation(size[:, t, :], diff[:, t, :], ACT.Abs, scale=gk_inv[:, t : t + 1])
         for t in range(PACK):
             nc.scalar.activation(big[t][:, :S], size[:, t, :], ACT.Ln, bias=consts[:, 0:1])
 
         larger = tile("larger", [P, PACK, S], F32, tag="kw")
-        st = [window("st%d" % t, WIN if t == 0 else WIDE) for t in range(PACK)]
-        other = [tile("other%d" % t, [P, S], F32, tag="sg%d" % (PACK - 1 - t)) for t in range(PACK)]
-        best = tile("best", [P, PACK, S], F32)
-        for t in range(PACK):
+        st = tile("st", [P, (PACK - 1) * S + WIDE], F32)
+        nc.gpsimd.memset(st[:, PACK * S :], 0.0)
+        other = tile("other", [P, PACK, S], F32)
+        for t in EARLY + LATE:
             pairs = big[t][:, 2 * S :].rearrange("p (j u) -> p j u", u=2)
             nc.vector.tensor_tensor(larger[:, t, :], pairs[:, :, 0], pairs[:, :, 1], ALU.max)
-            nc.vector.tensor_tensor(st[t][:, :S], y[t][:, :S], larger[:, t, :], ALU.subtract)
-            gather("s" if t == 0 else "v", other[t][:], st[t], n2_t[:])
-            nc.vector.tensor_tensor(best[:, t, :], st[t][:, :S], other[t][:], ALU.max)
+            nc.vector.tensor_tensor(st[:, t * S : (t + 1) * S], y[t][:, :S], larger[:, t, :], ALU.subtract)
+            nc.vector.tensor_copy(other[:, t, :], st[:, t * S : t * S + WIDE].indirect(n2_t[:]))
 
         inv = tile("inv", [P, PACK, S], F32, tag="size")
         for t in range(PACK):
@@ -238,8 +247,16 @@ def tile_picked_jkeyghopmhopnglse_none_po_kernel(
         zb = tile("zb", [P, S, PACK], BF16)
         zw = tile("zw", [P, S], U32)
         zs = tile("zs", [P, S], U8)
-        gains = gn_t[:].unsqueeze(1).unsqueeze(3).to_broadcast([P, S // 2, PACK, 2])
-        nc.vector.tensor_tensor(woven(zb[:]), planes(best[:]), gains, ALU.mult)
+        unsigned = tile("unsigned", [P, S, PACK], BF16)
+        st_planes = st[:, : PACK * S].rearrange("p (t j) -> p t j", t=PACK)
+        nc.vector.tensor_tensor(woven(unsigned[:]), planes(st_planes), planes(other[:]), ALU.max)
+        runs = S // SIGN_COLUMNS
+        nc.vector.tensor_tensor(
+            zb[:].rearrange("p (r j) t -> p r (j t)", r=runs),
+            unsigned[:].rearrange("p (r j) t -> p r (j t)", r=runs),
+            gn_sign[:].rearrange("p j t -> p (j t)").unsqueeze(1).to_broadcast([P, runs, SIGN_COLUMNS * PACK]),
+            ALU.mult,
+        )
         nc.vector.quantize_mx(out=zw[:].bitcast(FP8X4), scales=zs[:], in_=zb[:].rearrange("p j t -> p (j t)"))
         for u in range(2):
             for t in range(PACK):

@@ -26,7 +26,7 @@ CHUNK = 128
 SIGN_COLUMNS = 64
 EARLY = (3, 2)
 LATE = (1, 0)
-ON_VECTOR = (2, 2, 2, 2)
+ON_VECTOR = (2, 2, 3, 2)
 ORDER = (0, 2, 1, 3)
 
 FLOPS = 4 * 2 * 512 * 512 * 512
@@ -265,7 +265,7 @@ def tile_picked_jkeyghopmhopnglse_none_po_kernel(
         z2w = tile("z2w", [P, S], U32)
         z2s = tile("z2s", [P, S], U8)
         ex = [window("ex%d" % t) for t in range(PACK)]
-        h_kept = [tile("h_kept%d" % u, [P, PACK, HALF], F32) for u in range(2)]
+        h_kept = []
         ex_inv = tile("ex_inv", [P, PACK, HALF], F32)
 
         for u in range(2):
@@ -288,6 +288,7 @@ def tile_picked_jkeyghopmhopnglse_none_po_kernel(
         out_rows = out_0.rearrange("(p t) j -> p t j", t=PACK)
         out_words = out_1[0].rearrange("p n t -> p (n t)").bitcast(I32)
         chunks = [slice(CHUNK * c, CHUNK * (c + 1)) for c in range(S // CHUNK)]
+        h_kept.append(tile("h_kept", [P, PACK, HALF], F32, tag="zb"))
         for t in range(PACK):
             nc.vector.tensor_copy(h_kept[0][:, t, :], h_ps[0][t][:])
         before_log = {}
@@ -315,12 +316,13 @@ def tile_picked_jkeyghopmhopnglse_none_po_kernel(
                 before_log[c] = turned
                 continue
             quads = fetched[:].rearrange("p t j u -> p (t j) u")
-            twos = tile("twos%d" % c, [P, PACK * CHUNK, 2], F32, tag="twos")
-            nc.vector.tensor_tensor(twos[:], quads[:, :, 0:2], quads[:, :, 2:4], ALU.add)
+            twos = tile("twos%d" % c, [P, PACK * CHUNK, 2], F32, tag="twos%d" % c)
+            adder = nc.gpsimd if c == 2 else nc.vector
+            adder.tensor_tensor(twos[:], quads[:, :, 0:2], quads[:, :, 2:4], ALU.add)
             total = tile("total%d" % c, [P, PACK, CHUNK], F32)
-            nc.vector.tensor_tensor(total[:].rearrange("p t j -> p (t j)"), twos[:, :, 0], twos[:, :, 1], ALU.add)
+            adder.tensor_tensor(total[:].rearrange("p t j -> p (t j)"), twos[:, :, 0], twos[:, :, 1], ALU.add)
             ratio = tile("ratio%d" % c, [P, PACK, CHUNK], F32)
-            nc.vector.tensor_tensor(ratio[:], total[:], ex_inv[:, :, chunks[c - 2]], ALU.mult)
+            adder.tensor_tensor(ratio[:], total[:], ex_inv[:, :, chunks[c - 2]], ALU.mult)
             before_log[c] = ratio
         for c in (0, 1, 2, 3):
             cols = chunks[c]

@@ -15,19 +15,21 @@ ACT = mybir.ActivationFunctionType
 
 P = 128
 PACK = 4
+QUADRANTS = 4
 S = 512
 T = 1024
 G = 2048
-SPARE = 16
-WIN = S + SPARE
+ENTRIES = 16
+MEMBERS = 4
+WIN = S + 16
 WIDE = 704
 HALF = S // 2
 CHUNK = 128
 SIGN_COLUMNS = 64
 EARLY = (3, 2)
 LATE = (1, 0)
-ON_VECTOR = (2, 2, 3, 2)
-ORDER = (0, 2, 1, 3)
+N3_ON_VECTOR = 3
+LAST_ON_GPSIMD = 1
 
 FLOPS = 4 * 2 * 512 * 512 * 512
 
@@ -43,25 +45,33 @@ def tile_picked_jkeyghopmhopnglse_none_po_kernel(
         sb = ctx.enter_context(tc.tile_pool(name="sb", bufs=1))
         ps = ctx.enter_context(tc.psum_pool(name="ps", bufs=1))
 
-        def tile(name, shape, dtype, tag="", bufs=1):
-            return sb.tile(shape, dtype, name=name, tag=tag or name, bufs=bufs, align_bytes=64)
+        def tile(name, shape, dtype, tag=""):
+            return sb.tile(shape, dtype, name=name, tag=tag or name, bufs=1, align_bytes=64)
+
+        def bank(name, shape, number):
+            return ps.tile(shape, F32, name=name, tag="bank%d" % number)
 
         def load_list(name, src):
             held = lists.tile(list(src.shape), U16, name=name)
             nc.sync.dma_start(held[:], src)
             return held
 
-        def load_words(queue, name, src, tag=""):
+        def load_words(name, src, tag=""):
             held = tile(name, [P, src.shape[2]], I32, tag=tag)
-            queue.dma_start(held[:], src[0].rearrange("p n t -> p (n t)").bitcast(I32))
+            nc.sync.dma_start(held[:], src[0].rearrange("p n t -> p (n t)").bitcast(I32))
             return held
 
-        def load_scale_rows(queue, plane, first, src):
-            for q in range(4):
-                queue.dma_start(
+        def load_scale_rows(plane, first, src):
+            for q in range(QUADRANTS):
+                nc.sync.dma_start(
                     plane[32 * q + first : 32 * q + first + 4, :].bitcast(I32),
                     src[0, 4 * q : 4 * q + 4, :].bitcast(I32),
                 )
+
+        def load_gains(name, src):
+            held = tile(name, [P, PACK], F32)
+            nc.sync.dma_start(held[:], src.rearrange("(p t) o -> p (t o)", t=PACK))
+            return held
 
         def deal_words(name, src):
             dealt = tile(name, [P, S], I32)
@@ -84,21 +94,21 @@ def tile_picked_jkeyghopmhopnglse_none_po_kernel(
             nc.vector.tensor_copy(picked[:], table.indirect(offsets[:]))
             return picked
 
-        def gather(engine, out, window, offsets):
-            if engine == "v":
-                nc.vector.tensor_copy(out, window[:].indirect(offsets))
+        def gather(on_vector, out, source, offsets):
+            if on_vector:
+                nc.vector.tensor_copy(out, source[:].indirect(offsets))
             else:
-                nc.scalar.activation(out, window[:].indirect(offsets), ACT.Copy)
+                nc.scalar.activation(out, source[:].indirect(offsets), ACT.Copy)
 
         def window(name, width=WIN):
             held = tile(name, [P, width], F32)
             nc.gpsimd.memset(held[:, S:], 0.0)
             return held
 
-        def product(bank, cols, words, plane, t, moving_words, moving_plane, start, stop):
+        def product(out, cols, words, plane, t, moving_words, moving_plane, start, stop):
             rows = slice(P * t, P * (t + 1))
             nc.tensor.matmul_mx(
-                out=bank,
+                out=out,
                 lhsT=words[:, rows].bitcast(FP8X4),
                 lhsT_scale=plane[:, rows],
                 rhs=moving_words[:, cols].bitcast(FP8X4),
@@ -107,247 +117,266 @@ def tile_picked_jkeyghopmhopnglse_none_po_kernel(
                 stop=stop,
             )
 
+        def quantise(words, plane, woven_values):
+            nc.vector.quantize_mx(
+                out=words.bitcast(FP8X4), scales=plane, in_=woven_values.rearrange("p j t -> p (j t)")
+            )
+
         def woven(ap):
             return ap.rearrange("p (c i) t -> p c t i", i=2)
 
-        def planes(ap):
+        def by_tiles(ap):
             return ap.rearrange("p t (c i) -> p c t i", i=2)
 
-        xs = tile("xs", [P, T], U8)
-        nc.gpsimd.memset(xs[:].bitcast(I32), 0)
-        w1s = tile("w1s", [P, S], U8)
-        nc.vector.memset(w1s[:].bitcast(I32), 0)
-        ds = tile("ds", [P, G], U8)
-        nc.vector.memset(ds[:].bitcast(I32), 0)
+        x_plane = tile("x_plane", [P, T], U8)
+        nc.gpsimd.memset(x_plane[:].bitcast(I32), 0)
+        w1_plane = tile("w1_plane", [P, S], U8)
+        nc.vector.memset(w1_plane[:].bitcast(I32), 0)
+        d_rows = tile("d_rows", [P, G], U8)
+        nc.vector.memset(d_rows[:].bitcast(I32), 0)
         key_plane = tile("key_plane", [P, S], U8)
         nc.gpsimd.memset(key_plane[:].bitcast(I32), 0)
-        consts = tile("consts", [P, 2], F32)
-        nc.gpsimd.memset(consts[:, 0:1], 8.0)
-        nc.gpsimd.memset(consts[:, 1:2], 1.0)
+        biases = tile("biases", [P, 2], F32)
+        eight, one = biases[:, 0:1], biases[:, 1:2]
+        nc.gpsimd.memset(eight, 8.0)
+        nc.gpsimd.memset(one, 1.0)
 
         ident = tile("ident", [P, P], F32)
         make_identity(nc, ident[:])
 
         unread = tile("unread", [P, 1], F32)
-        nc.scalar.activation(unread[:], consts[:, 1:2], ACT.Ln)
+        nc.scalar.activation(unread[:], one, ACT.Ln)
 
         offs_t = load_list("offs_t", offs)
-        xw = load_words(nc.sync, "xw", x_words)
-        load_scale_rows(nc.sync, xs, 0, x_scales)
-        w1w = load_words(nc.sync, "w1w", w1_words)
-        load_scale_rows(nc.sync, w1s, 0, w1_scales)
-        gn_t = tile("gn_t", [P, PACK], F32)
-        nc.sync.dma_start(gn_t[:], gn.rearrange("(p t) o -> p (t o)", t=PACK))
+        xw = load_words("xw", x_words)
+        load_scale_rows(x_plane, 0, x_scales)
+        w1w = load_words("w1w", w1_words)
+        load_scale_rows(w1_plane, 0, w1_scales)
+        gn_t = load_gains("gn_t", gn)
         gn_size = tile("gn_size", [P, PACK], F32)
         nc.scalar.activation(gn_size[:], gn_t[:], ACT.Abs)
         gn_sign = tile("gn_sign", [P, SIGN_COLUMNS, PACK], BF16)
         nc.scalar.activation(gn_sign[:], gn_t[:].unsqueeze(1).to_broadcast([P, SIGN_COLUMNS, PACK]), ACT.Sign)
         kidx_t = load_list("kidx_t", kidx)
-        nc.sync.dma_start(ds[0:P:8, :].bitcast(I32), d_scales[0].bitcast(I32))
+        nc.sync.dma_start(d_rows[0:P:8, :].bitcast(I32), d_scales[0].bitcast(I32))
         n1_t = load_list("n1_t", n1)
         two_t = load_list("two_t", two)
-        dw = load_words(nc.sync, "dw", d_words)
-        gk_t = tile("gk_t", [P, PACK], F32)
-        nc.sync.dma_start(gk_t[:], gk.rearrange("(p t) o -> p (t o)", t=PACK))
+        dw = load_words("dw", d_words)
+        gk_t = load_gains("gk_t", gk)
         n3_t = load_list("n3_t", n3)
         n2_t = load_list("n2_t", n2)
         n4_t = load_list("n4_t", n4)
         n5_t = load_list("n5_t", n5)
 
-        x1w = pick("x1w", xw[:].bitcast(U32), offs_t, U32)
-        x1s = pick("x1s", xs[:], offs_t, U8)
-        w1d = deal_words("w1d", w1w[:])
-        w1p = deal_bytes("w1p", w1s[:])
+        x1_words = pick("x1_words", xw[:].bitcast(U32), offs_t, U32)
+        x1_plane = pick("x1_plane", x_plane[:], offs_t, U8)
+        w1_dealt = deal_words("w1_dealt", w1w[:])
+        w1_dealt_plane = deal_bytes("w1_dealt_plane", w1_plane[:])
         everything = slice(0, S)
-        y_ps = {t: ps.tile([P, S], F32, name="y%d" % t, tag="bank%d" % t) for t in EARLY}
+        y_ps = {t: bank("y%d" % t, [P, S], t) for t in EARLY}
         for t in EARLY:
-            product(y_ps[t][:], everything, w1d, w1p, t, x1w, x1s, True, True)
+            product(y_ps[t][:], everything, w1_dealt, w1_dealt_plane, t, x1_words, x1_plane, True, True)
 
-        big = [tile("big%d" % t, [P, 4 * S], F32) for t in range(PACK)]
-        y = [window("yw%d" % t) for t in range(PACK)]
+        wide = [tile("wide%d" % t, [P, 4 * S], F32) for t in range(PACK)]
+        log_size = [wide[t][:, :S] for t in range(PACK)]
+        s_at_n3 = [wide[t][:, S : 2 * S] for t in range(PACK)]
+        y_members = [wide[t][:, 2 * S :] for t in range(PACK)]
+        y = [window("y_window%d" % t) for t in range(PACK)]
+        span = S // ENTRIES
 
-        def members(engine, t):
+        def keep_y(t, source):
+            nc.scalar.activation(y[t][:, :S], source[:], ACT.Copy, scale=gn_size[:, t : t + 1])
+
+        def fetch_members(on_vector, t):
             for u in range(2):
-                gather(engine, big[t][:, (2 + u) * S : (3 + u) * S], y[t], n1_t[:, 32 * u : 32 * (u + 1)])
+                gather(on_vector, y_members[t][:, u * S : (u + 1) * S], y[t], n1_t[:, span * u : span * (u + 1)])
 
         for t in EARLY:
-            nc.scalar.activation(y[t][:, :S], y_ps[t][:], ACT.Copy, scale=gn_size[:, t : t + 1])
-            members("s", t)
+            keep_y(t, y_ps[t])
+            fetch_members(False, t)
 
-        ks = pick("ks", ds[:], kidx_t, U8)
-        ksd = deal_bytes("ksd", ks[:])
-        for q in range(4):
+        key_rows = pick("key_rows", d_rows[:], kidx_t, U8)
+        key_rows_dealt = deal_bytes("key_rows_dealt", key_rows[:])
+        for q in range(QUADRANTS):
             nc.sync.dma_start(
                 key_plane[32 * q : 32 * q + 4, :].bitcast(I32),
-                ksd[32 * q : 32 * q + 32 : 8, :].bitcast(I32),
+                key_rows_dealt[32 * q : 32 * q + 32 : 8, :].bitcast(I32),
             )
-        x2w = pick("x2w", xw[:].bitcast(U32), two_t, U32, tag="ks")
-        x2s = pick("x2s", xs[:], two_t, U8)
-        kw = pick("kw", dw[:].bitcast(U32), kidx_t, U32)
-        kwd = deal_words("kwd", kw[:].bitcast(I32))
-        s_ps = [ps.tile([P, S], F32, name="s%d" % t, tag="bank%d" % (PACK + t)) for t in range(PACK)]
+        x2_words = pick("x2_words", xw[:].bitcast(U32), two_t, U32, tag="key_rows")
+        x2_plane = pick("x2_plane", x_plane[:], two_t, U8)
+        key_words = pick("key_words", dw[:].bitcast(U32), kidx_t, U32)
+        key_dealt = deal_words("key_dealt", key_words[:].bitcast(I32))
+        s_ps = [bank("s%d" % t, [P, S], PACK + t) for t in range(PACK)]
         for t in range(PACK):
-            product(s_ps[t][:], everything, kwd, key_plane, t, x2w, x2s, True, True)
+            product(s_ps[t][:], everything, key_dealt, key_plane, t, x2_words, x2_plane, True, True)
 
-        w2w = load_words(nc.sync, "w2w", w2_words, tag="xw")
-        w3w = load_words(nc.sync, "w3w", w3_words, tag="dw")
-        w23s = tile("w23s", [P, S], U8, tag="ksd")
-        nc.gpsimd.memset(w23s[:].bitcast(I32), 0)
-        load_scale_rows(nc.sync, w23s, 0, w2_scales)
-        load_scale_rows(nc.sync, w23s, 4, w3_scales)
+        w2w = load_words("w2w", w2_words, tag="xw")
+        w3w = load_words("w3w", w3_words, tag="dw")
+        w23_plane = tile("w23_plane", [P, S], U8, tag="key_rows_dealt")
+        nc.gpsimd.memset(w23_plane[:].bitcast(I32), 0)
+        load_scale_rows(w23_plane, 0, w2_scales)
+        load_scale_rows(w23_plane, 4, w3_scales)
 
         gk_safe = tile("gk_safe", [P, PACK], F32)
         nc.vector.scalar_tensor_tensor(gk_safe[:], gk_t[:], 0.0, gk_t[:], ALU.is_equal, ALU.add)
         gk_inv = tile("gk_inv", [P, PACK], F32)
         nc.vector.reciprocal(gk_inv[:], gk_safe[:])
 
-        sg = [window("sg%d" % t, WIDE if t in (3,) else WIN) for t in range(PACK)]
+        s_gained = [window("s_window%d" % t, WIDE if t == N3_ON_VECTOR else WIN) for t in range(PACK)]
         diff = tile("diff", [P, PACK, S], F32)
-        size = tile("size", [P, PACK, S], F32, tag="size")
+        size = tile("size", [P, PACK, S], F32)
         for t in range(PACK):
-            nc.scalar.activation(sg[t][:, :S], s_ps[t][:], ACT.Copy, scale=gk_t[:, t : t + 1])
-            gather("v" if t in (3,) else "s", big[t][:, S : 2 * S], sg[t], n3_t[:])
+            nc.scalar.activation(s_gained[t][:, :S], s_ps[t][:], ACT.Copy, scale=gk_t[:, t : t + 1])
+            gather(t == N3_ON_VECTOR, s_at_n3[t], s_gained[t], n3_t[:])
             nc.vector.scalar_tensor_tensor(
-                diff[:, t, :], s_ps[t][:], gk_t[:, t : t + 1], big[t][:, S : 2 * S], ALU.mult, ALU.subtract
+                diff[:, t, :], s_ps[t][:], gk_t[:, t : t + 1], s_at_n3[t], ALU.mult, ALU.subtract
             )
+
         for n, t in enumerate(LATE):
-            late = ps.tile([P, S], F32, name="y%d" % t, tag="bank%d" % (PACK + n))
-            product(late[:], everything, w1d, w1p, t, x1w, x1s, True, True)
-            nc.scalar.activation(y[t][:, :S], late[:], ACT.Copy, scale=gn_size[:, t : t + 1])
-        members("s", LATE[1])
-        members("v", LATE[0])
+            y_late = bank("y%d" % t, [P, S], PACK + n)
+            product(y_late[:], everything, w1_dealt, w1_dealt_plane, t, x1_words, x1_plane, True, True)
+            keep_y(t, y_late)
+        fetch_members(False, LATE[1])
+        fetch_members(True, LATE[0])
+
         for t in range(PACK):
             nc.scalar.activation(size[:, t, :], diff[:, t, :], ACT.Abs, scale=gk_inv[:, t : t + 1])
         for t in range(PACK):
-            nc.scalar.activation(big[t][:, :S], size[:, t, :], ACT.Ln, bias=consts[:, 0:1])
+            nc.scalar.activation(log_size[t], size[:, t, :], ACT.Ln, bias=eight)
 
-        larger = tile("larger", [P, PACK, S], F32, tag="kw")
+        larger = tile("larger", [P, PACK, S], F32, tag="key_words")
         st = tile("st", [P, (PACK - 1) * S + WIDE], F32)
         nc.gpsimd.memset(st[:, PACK * S :], 0.0)
-        other = tile("other", [P, PACK, S], F32)
+        st_at_n2 = tile("st_at_n2", [P, PACK, S], F32)
         for t in EARLY + LATE:
-            pairs = big[t][:, 2 * S :].rearrange("p (j u) -> p j u", u=2)
+            pairs = y_members[t].rearrange("p (j u) -> p j u", u=2)
             nc.vector.tensor_tensor(larger[:, t, :], pairs[:, :, 0], pairs[:, :, 1], ALU.max)
             nc.vector.tensor_tensor(st[:, t * S : (t + 1) * S], y[t][:, :S], larger[:, t, :], ALU.subtract)
-            nc.vector.tensor_copy(other[:, t, :], st[:, t * S : t * S + WIDE].indirect(n2_t[:]))
+            nc.vector.tensor_copy(st_at_n2[:, t, :], st[:, t * S : t * S + WIDE].indirect(n2_t[:]))
 
-        inv = tile("inv", [P, PACK, S], F32, tag="size")
+        inverse = tile("inverse", [P, PACK, S], F32, tag="size")
         for t in range(PACK):
-            nc.scalar.activation(inv[:, t, :], big[t][:].indirect(n4_t[:]), ACT.Exp, scale=-1.0)
+            nc.scalar.activation(inverse[:, t, :], wide[t][:].indirect(n4_t[:]), ACT.Exp, scale=-1.0)
 
-        w2d = deal_words("w2d", w2w[:])
-        w3d = deal_words("w3d", w3w[:])
-        w23p = deal_bytes("w23p", w23s[:])
+        w2_dealt = deal_words("w2_dealt", w2w[:])
+        w3_dealt = deal_words("w3_dealt", w3w[:])
+        w23_dealt_plane = deal_bytes("w23_dealt_plane", w23_plane[:])
 
         halves = [slice(HALF * u, HALF * (u + 1)) for u in range(2)]
-        h_ps = [
-            [ps.tile([P, HALF], F32, name="h%d%d" % (u, t), tag="bank%d" % (PACK * u + t)) for t in range(PACK)]
-            for u in range(2)
-        ]
-        zb = tile("zb", [P, S, PACK], BF16)
-        zw = tile("zw", [P, S], U32)
-        zs = tile("zs", [P, S], U8)
+        h_ps = [[bank("h%d%d" % (u, t), [P, HALF], PACK * u + t) for t in range(PACK)] for u in range(2)]
+        z_woven = tile("z_woven", [P, S, PACK], BF16)
+        z_words = tile("z_words", [P, S], U32)
+        z_plane = tile("z_plane", [P, S], U8)
         unsigned = tile("unsigned", [P, S, PACK], BF16)
-        st_planes = st[:, : PACK * S].rearrange("p (t j) -> p t j", t=PACK)
-        nc.vector.tensor_tensor(woven(unsigned[:]), planes(st_planes), planes(other[:]), ALU.max)
+        st_tiles = st[:, : PACK * S].rearrange("p (t j) -> p t j", t=PACK)
+        nc.vector.tensor_tensor(woven(unsigned[:]), by_tiles(st_tiles), by_tiles(st_at_n2[:]), ALU.max)
         runs = S // SIGN_COLUMNS
         nc.vector.tensor_tensor(
-            zb[:].rearrange("p (r j) t -> p r (j t)", r=runs),
+            z_woven[:].rearrange("p (r j) t -> p r (j t)", r=runs),
             unsigned[:].rearrange("p (r j) t -> p r (j t)", r=runs),
             gn_sign[:].rearrange("p j t -> p (j t)").unsqueeze(1).to_broadcast([P, runs, SIGN_COLUMNS * PACK]),
             ALU.mult,
         )
-        nc.vector.quantize_mx(out=zw[:].bitcast(FP8X4), scales=zs[:], in_=zb[:].rearrange("p j t -> p (j t)"))
+        quantise(z_words[:], z_plane[:], z_woven[:])
         for u in range(2):
             for t in range(PACK):
-                product(h_ps[u][t][:], halves[u], w2d, w23p, t, zw, zs, True, False)
+                product(h_ps[u][t][:], halves[u], w2_dealt, w23_dealt_plane, t, z_words, z_plane, True, False)
 
-        z2w = tile("z2w", [P, S], U32)
-        z2s = tile("z2s", [P, S], U8)
-        ex = [window("ex%d" % t) for t in range(PACK)]
-        h_kept = []
+        z2_words = tile("z2_words", [P, S], U32)
+        z2_plane = tile("z2_plane", [P, S], U8)
+        ex = [window("ex_window%d" % t) for t in range(PACK)]
         ex_inv = tile("ex_inv", [P, PACK, HALF], F32)
 
         for u in range(2):
-            z2b = tile("z2b%d" % u, [P, HALF, PACK], BF16, tag="zb")
+            z2_woven = tile("z2_woven%d" % u, [P, HALF, PACK], BF16, tag="z_woven")
             nc.vector.tensor_tensor(
-                woven(z2b[:]), planes(diff[:, :, halves[u]]), planes(inv[:, :, halves[u]]), ALU.mult
+                woven(z2_woven[:]), by_tiles(diff[:, :, halves[u]]), by_tiles(inverse[:, :, halves[u]]), ALU.mult
             )
-            nc.vector.quantize_mx(
-                out=z2w[:, halves[u]].bitcast(FP8X4),
-                scales=z2s[:, halves[u]],
-                in_=z2b[:].rearrange("p j t -> p (j t)"),
-            )
+            quantise(z2_words[:, halves[u]], z2_plane[:, halves[u]], z2_woven[:])
             for t in range(PACK):
-                product(h_ps[u][t][:], halves[u], w3d, w23p[4:P, :], t, z2w, z2s, False, True)
+                product(
+                    h_ps[u][t][:], halves[u], w3_dealt, w23_dealt_plane[4:P, :], t, z2_words, z2_plane, False, True
+                )
             for t in range(PACK):
                 nc.scalar.activation(ex[t][:, halves[u]], h_ps[u][t][:], ACT.Exp)
 
-        ow = tile("ow", [P, S], U32)
-        osc = tile("osc", [P, S], U8)
+        out_codes = tile("out_codes", [P, S], U32)
+        out_plane = tile("out_plane", [P, S], U8)
         out_rows = out_0.rearrange("(p t) j -> p t j", t=PACK)
         out_words = out_1[0].rearrange("p n t -> p (n t)").bitcast(I32)
         chunks = [slice(CHUNK * c, CHUNK * (c + 1)) for c in range(S // CHUNK)]
-        h_kept.append(tile("h_kept", [P, PACK, HALF], F32, tag="zb"))
+        per_half = HALF // CHUNK
+        h_low = tile("h_low", [P, PACK, HALF], F32, tag="z_woven")
         for t in range(PACK):
-            nc.vector.tensor_copy(h_kept[0][:, t, :], h_ps[0][t][:])
+            nc.vector.tensor_copy(h_low[:, t, :], h_ps[0][t][:])
+        fetched = [tile("fetched%d" % c, [P, PACK, CHUNK, MEMBERS], F32) for c in range(len(chunks))]
         before_log = {}
-        for c in ORDER:
-            cols = chunks[c]
-            fetched = tile("fetched%d" % c, [P, PACK, CHUNK, 4], F32)
-            for t in range(PACK):
-                gather(
-                    "v" if t < ON_VECTOR[c] else "s",
-                    fetched[:, t, :, :].rearrange("p j u -> p (j u)"),
-                    ex[t],
-                    n5_t[:, 32 * c : 32 * (c + 1)],
-                )
-            if c == 0:
-                for t in range(PACK):
-                    nc.scalar.activation(ex_inv[:, t, :], h_ps[1][t][:], ACT.Exp, scale=-1.0)
-            if c < 2:
-                turned = ps.tile([P, PACK, CHUNK], F32, name="turned%d" % c, tag="bank%d" % c)
-                for t in range(PACK):
-                    terms = [ex[t][:, cols]] + [fetched[:, t, :, u] for u in range(4)]
-                    for n, term in enumerate(terms):
-                        nc.tensor.matmul(
-                            turned[:, t, :], term, ident[:], is_transpose=True, start=n == 0, stop=n == 4
-                        )
-                before_log[c] = turned
-                continue
-            quads = fetched[:].rearrange("p t j u -> p (t j) u")
-            twos = tile("twos%d" % c, [P, PACK * CHUNK, 2], F32, tag="twos%d" % c)
-            adder = nc.gpsimd if c == 2 else nc.vector
+
+        def fetch_ex(on_vector, c, t):
+            gather(
+                on_vector,
+                fetched[c][:, t, :, :].rearrange("p j u -> p (j u)"),
+                ex[t],
+                n5_t[:, span * c : span * (c + 1)],
+            )
+
+        for c in range(per_half):
+            before_log[c] = bank("turned%d" % c, [P, PACK, CHUNK], c)
+        for t in range(PACK):
+            for c in range(per_half):
+                fetch_ex(True, c, t)
+                terms = [ex[t][:, chunks[c]]] + [fetched[c][:, t, :, u] for u in range(MEMBERS)]
+                for n, term in enumerate(terms):
+                    nc.tensor.matmul(
+                        before_log[c][:, t, :], term, ident[:], is_transpose=True, start=n == 0, stop=n == MEMBERS
+                    )
+
+        def add_members(adder, c, lo, hi):
+            quads = fetched[c][:, lo:hi, :, :].rearrange("p t j u -> p (t j) u")
+            twos = tile("twos%d%d" % (c, lo), [P, (hi - lo) * CHUNK, 2], F32)
             adder.tensor_tensor(twos[:], quads[:, :, 0:2], quads[:, :, 2:4], ALU.add)
-            total = tile("total%d" % c, [P, PACK, CHUNK], F32)
+            total = tile("total%d%d" % (c, lo), [P, hi - lo, CHUNK], F32)
             adder.tensor_tensor(total[:].rearrange("p t j -> p (t j)"), twos[:, :, 0], twos[:, :, 1], ALU.add)
-            ratio = tile("ratio%d" % c, [P, PACK, CHUNK], F32)
-            adder.tensor_tensor(ratio[:], total[:], ex_inv[:, :, chunks[c - 2]], ALU.mult)
-            before_log[c] = ratio
-        for c in (0, 1, 2, 3):
-            cols = chunks[c]
-            result = tile("result%d" % c, [P, PACK, CHUNK], F32)
-            if c < 2:
+            adder.tensor_tensor(
+                before_log[c][:, lo:hi, :], total[:], ex_inv[:, lo:hi, chunks[c - per_half]], ALU.mult
+            )
+
+        third, last = per_half, per_half + 1
+        for t in range(PACK):
+            fetch_ex(False, third, t)
+        for t in range(PACK):
+            nc.scalar.activation(ex_inv[:, t, :], h_ps[1][t][:], ACT.Exp, scale=-1.0)
+        before_log[third] = tile("ratio%d" % third, [P, PACK, CHUNK], F32)
+        add_members(nc.gpsimd, third, 0, PACK // 2)
+        add_members(nc.gpsimd, third, PACK // 2, PACK)
+        for t in range(PACK):
+            fetch_ex(t == PACK - 1, last, t)
+        before_log[last] = tile("ratio%d" % last, [P, PACK, CHUNK], F32)
+        add_members(nc.gpsimd, last, 0, LAST_ON_GPSIMD)
+        add_members(nc.vector, last, LAST_ON_GPSIMD, PACK)
+
+        for c, cols in enumerate(chunks):
+            result = tile("result%d" % c, [P, PACK, CHUNK], F32, tag="fetched%d" % (c - 1) if c == third else "")
+            rounded = tile("rounded%d" % c, [P, CHUNK, PACK], BF16)
+            if c < per_half:
                 logs = tile("logs%d" % c, [P, PACK, CHUNK], F32)
                 nc.scalar.activation(logs[:], before_log[c][:], ACT.Ln)
-                back = ps.tile([P, PACK, CHUNK], F32, name="back%d" % c, tag="bank%d" % (2 + c))
+                back = bank("back%d" % c, [P, PACK, CHUNK], per_half + c)
                 for t in range(PACK):
                     nc.tensor.transpose(back[:, t, :], logs[:, t, :], ident[:])
-                nc.vector.tensor_tensor(result[:], back[:], h_kept[c // 2][:, :, chunks[c % 2]], ALU.subtract)
+                nc.vector.tensor_tensor(result[:], back[:], h_low[:, :, cols], ALU.subtract)
+                round_once = nc.vector.tensor_copy
             else:
-                nc.scalar.activation(result[:], before_log[c][:], ACT.Ln, bias=consts[:, 1:2])
+                nc.scalar.activation(result[:], before_log[c][:], ACT.Ln, bias=one)
+                round_once = nc.scalar.copy
             nc.sync.dma_start(out_rows[:, :, cols], result[:])
-            rounded = tile("rounded%d" % c, [P, CHUNK, PACK], BF16)
-            if c in (2, 3):
-                nc.scalar.copy(woven(rounded[:]), planes(result[:]))
-            else:
-                nc.vector.tensor_copy(woven(rounded[:]), planes(result[:]))
-            nc.vector.quantize_mx(
-                out=ow[:, cols].bitcast(FP8X4), scales=osc[:, cols], in_=rounded[:].rearrange("p j t -> p (j t)")
-            )
-            if c % 2:
-                nc.sync.dma_start(out_words[:, halves[c // 2]], ow[:, halves[c // 2]].bitcast(I32))
-        for q in range(4):
-            (nc.sync if q < 2 else nc.scalar).dma_start(
-                out_2[0, 4 * q : 4 * q + 4, :].bitcast(I32), osc[32 * q : 32 * q + 4, :].bitcast(I32)
+            round_once(woven(rounded[:]), by_tiles(result[:]))
+            quantise(out_codes[:, cols], out_plane[:, cols], rounded[:])
+            if c % per_half == per_half - 1:
+                done = halves[c // per_half]
+                nc.sync.dma_start(out_words[:, done], out_codes[:, done].bitcast(I32))
+        for q in range(QUADRANTS):
+            queue = nc.sync if q < QUADRANTS // 2 else nc.scalar
+            queue.dma_start(
+                out_2[0, 4 * q : 4 * q + 4, :].bitcast(I32), out_plane[32 * q : 32 * q + 4, :].bitcast(I32)
             )

from contextlib import ExitStack

import concourse.mybir as mybir
from concourse.masks import make_identity

F32 = mybir.dt.float32
BF16 = mybir.dt.bfloat16
I32 = mybir.dt.int32
U32 = mybir.dt.uint32
U16 = mybir.dt.uint16
U8 = mybir.dt.uint8
FP8X4 = mybir.dt.float8_e4m3fn_x4
ALU = mybir.AluOpType
ACT = mybir.ActivationFunctionType

P = 128
PACK = 4
QUADRANTS = 4
S = 512
T = 1024
G = 2048
ENTRIES = 16
MEMBERS = 4
WIN = S + 16
WIDE = 704
HALF = S // 2
CHUNK = 128
SIGN_COLUMNS = 64
EARLY = (3, 2)
LATE = (1, 0)
N3_ON_VECTOR = 3
LAST_ON_GPSIMD = 1

FLOPS = 4 * 2 * 512 * 512 * 512


def tile_picked_jkeyghopmhopnglse_none_po_kernel(
    tc, x_words, x_scales, w1_words, w1_scales, d_words, d_scales, gn, gk,
    w2_words, w2_scales, w3_words, w3_scales, offs, kidx, two, n1, n2, n3, n4, n5,
    out_0, out_1, out_2,
):
    nc = tc.nc
    with ExitStack() as ctx:
        lists = ctx.enter_context(tc.tile_pool(name="lists", bufs=1))
        sb = ctx.enter_context(tc.tile_pool(name="sb", bufs=1))
        ps = ctx.enter_context(tc.psum_pool(name="ps", bufs=1))

        def tile(name, shape, dtype, tag=""):
            return sb.tile(shape, dtype, name=name, tag=tag or name, bufs=1, align_bytes=64)

        def bank(name, shape, number):
            return ps.tile(shape, F32, name=name, tag="bank%d" % number)

        def load_list(name, src):
            held = lists.tile(list(src.shape), U16, name=name)
            nc.sync.dma_start(held[:], src)
            return held

        def load_words(name, src, tag=""):
            held = tile(name, [P, src.shape[2]], I32, tag=tag)
            nc.sync.dma_start(held[:], src[0].rearrange("p n t -> p (n t)").bitcast(I32))
            return held

        def load_scale_rows(plane, first, src):
            for q in range(QUADRANTS):
                nc.sync.dma_start(
                    plane[32 * q + first : 32 * q + first + 4, :].bitcast(I32),
                    src[0, 4 * q : 4 * q + 4, :].bitcast(I32),
                )

        def load_gains(name, src):
            held = tile(name, [P, PACK], F32)
            nc.sync.dma_start(held[:], src.rearrange("(p t) o -> p (t o)", t=PACK))
            return held

        def deal_words(name, src):
            dealt = tile(name, [P, S], I32)
            nc.vector.tensor_copy(
                dealt[:].rearrange("p (t c i) -> p c t i", t=PACK, i=4),
                src.rearrange("p (c i t) -> p c t i", t=PACK, i=4),
            )
            return dealt

        def deal_bytes(name, src):
            dealt = tile(name, [P, S], U8)
            nc.vector.tensor_copy(
                dealt[:].rearrange("p (t m) -> p t m", t=PACK),
                src.rearrange("p (m t) -> p t m", t=PACK),
            )
            return dealt

        def pick(name, table, offsets, dtype, tag=""):
            picked = tile(name, [P, S], dtype, tag=tag)
            nc.vector.tensor_copy(picked[:], table.indirect(offsets[:]))
            return picked

        def gather(on_vector, out, source, offsets):
            if on_vector:
                nc.vector.tensor_copy(out, source[:].indirect(offsets))
            else:
                nc.scalar.activation(out, source[:].indirect(offsets), ACT.Copy)

        def window(name, width=WIN):
            held = tile(name, [P, width], F32)
            nc.gpsimd.memset(held[:, S:], 0.0)
            return held

        def product(out, cols, words, plane, t, moving_words, moving_plane, start, stop):
            rows = slice(P * t, P * (t + 1))
            nc.tensor.matmul_mx(
                out=out,
                lhsT=words[:, rows].bitcast(FP8X4),
                lhsT_scale=plane[:, rows],
                rhs=moving_words[:, cols].bitcast(FP8X4),
                rhs_scale=moving_plane[:, cols],
                start=start,
                stop=stop,
            )

        def quantise(words, plane, woven_values):
            nc.vector.quantize_mx(
                out=words.bitcast(FP8X4), scales=plane, in_=woven_values.rearrange("p j t -> p (j t)")
            )

        def woven(ap):
            return ap.rearrange("p (c i) t -> p c t i", i=2)

        def by_tiles(ap):
            return ap.rearrange("p t (c i) -> p c t i", i=2)

        x_plane = tile("x_plane", [P, T], U8)
        nc.gpsimd.memset(x_plane[:].bitcast(I32), 0)
        w1_plane = tile("w1_plane", [P, S], U8)
        nc.vector.memset(w1_plane[:].bitcast(I32), 0)
        d_rows = tile("d_rows", [P, G], U8)
        nc.vector.memset(d_rows[:].bitcast(I32), 0)
        key_plane = tile("key_plane", [P, S], U8)
        nc.gpsimd.memset(key_plane[:].bitcast(I32), 0)
        biases = tile("biases", [P, 2], F32)
        eight, one = biases[:, 0:1], biases[:, 1:2]
        nc.gpsimd.memset(eight, 8.0)
        nc.gpsimd.memset(one, 1.0)

        ident = tile("ident", [P, P], F32)
        make_identity(nc, ident[:])

        unread = tile("unread", [P, 1], F32)
        nc.scalar.activation(unread[:], one, ACT.Ln)

        offs_t = load_list("offs_t", offs)
        xw = load_words("xw", x_words)
        load_scale_rows(x_plane, 0, x_scales)
        w1w = load_words("w1w", w1_words)
        load_scale_rows(w1_plane, 0, w1_scales)
        gn_t = load_gains("gn_t", gn)
        gn_size = tile("gn_size", [P, PACK], F32)
        nc.scalar.activation(gn_size[:], gn_t[:], ACT.Abs)
        gn_sign = tile("gn_sign", [P, SIGN_COLUMNS, PACK], BF16)
        nc.scalar.activation(gn_sign[:], gn_t[:].unsqueeze(1).to_broadcast([P, SIGN_COLUMNS, PACK]), ACT.Sign)
        kidx_t = load_list("kidx_t", kidx)
        nc.sync.dma_start(d_rows[0:P:8, :].bitcast(I32), d_scales[0].bitcast(I32))
        n1_t = load_list("n1_t", n1)
        two_t = load_list("two_t", two)
        dw = load_words("dw", d_words)
        gk_t = load_gains("gk_t", gk)
        n3_t = load_list("n3_t", n3)
        n2_t = load_list("n2_t", n2)
        n4_t = load_list("n4_t", n4)
        n5_t = load_list("n5_t", n5)

        x1_words = pick("x1_words", xw[:].bitcast(U32), offs_t, U32)
        x1_plane = pick("x1_plane", x_plane[:], offs_t, U8)
        w1_dealt = deal_words("w1_dealt", w1w[:])
        w1_dealt_plane = deal_bytes("w1_dealt_plane", w1_plane[:])
        everything = slice(0, S)
        y_ps = {t: bank("y%d" % t, [P, S], t) for t in EARLY}
        for t in EARLY:
            product(y_ps[t][:], everything, w1_dealt, w1_dealt_plane, t, x1_words, x1_plane, True, True)

        wide = [tile("wide%d" % t, [P, 4 * S], F32) for t in range(PACK)]
        log_size = [wide[t][:, :S] for t in range(PACK)]
        s_at_n3 = [wide[t][:, S : 2 * S] for t in range(PACK)]
        y_members = [wide[t][:, 2 * S :] for t in range(PACK)]
        y = [window("y_window%d" % t) for t in range(PACK)]
        span = S // ENTRIES

        def keep_y(t, source):
            nc.scalar.activation(y[t][:, :S], source[:], ACT.Copy, scale=gn_size[:, t : t + 1])

        def fetch_members(on_vector, t):
            for u in range(2):
                gather(on_vector, y_members[t][:, u * S : (u + 1) * S], y[t], n1_t[:, span * u : span * (u + 1)])

        for t in EARLY:
            keep_y(t, y_ps[t])
            fetch_members(False, t)

        key_rows = pick("key_rows", d_rows[:], kidx_t, U8)
        key_rows_dealt = deal_bytes("key_rows_dealt", key_rows[:])
        for q in range(QUADRANTS):
            nc.sync.dma_start(
                key_plane[32 * q : 32 * q + 4, :].bitcast(I32),
                key_rows_dealt[32 * q : 32 * q + 32 : 8, :].bitcast(I32),
            )
        x2_words = pick("x2_words", xw[:].bitcast(U32), two_t, U32, tag="key_rows")
        x2_plane = pick("x2_plane", x_plane[:], two_t, U8)
        key_words = pick("key_words", dw[:].bitcast(U32), kidx_t, U32)
        key_dealt = deal_words("key_dealt", key_words[:].bitcast(I32))
        s_ps = [bank("s%d" % t, [P, S], PACK + t) for t in range(PACK)]
        for t in range(PACK):
            product(s_ps[t][:], everything, key_dealt, key_plane, t, x2_words, x2_plane, True, True)

        w2w = load_words("w2w", w2_words, tag="xw")
        w3w = load_words("w3w", w3_words, tag="dw")
        w23_plane = tile("w23_plane", [P, S], U8, tag="key_rows_dealt")
        nc.gpsimd.memset(w23_plane[:].bitcast(I32), 0)
        load_scale_rows(w23_plane, 0, w2_scales)
        load_scale_rows(w23_plane, 4, w3_scales)

        gk_safe = tile("gk_safe", [P, PACK], F32)
        nc.vector.scalar_tensor_tensor(gk_safe[:], gk_t[:], 0.0, gk_t[:], ALU.is_equal, ALU.add)
        gk_inv = tile("gk_inv", [P, PACK], F32)
        nc.vector.reciprocal(gk_inv[:], gk_safe[:])

        s_gained = [window("s_window%d" % t, WIDE if t == N3_ON_VECTOR else WIN) for t in range(PACK)]
        diff = tile("diff", [P, PACK, S], F32)
        size = tile("size", [P, PACK, S], F32)
        for t in range(PACK):
            nc.scalar.activation(s_gained[t][:, :S], s_ps[t][:], ACT.Copy, scale=gk_t[:, t : t + 1])
            gather(t == N3_ON_VECTOR, s_at_n3[t], s_gained[t], n3_t[:])
            nc.vector.scalar_tensor_tensor(
                diff[:, t, :], s_ps[t][:], gk_t[:, t : t + 1], s_at_n3[t], ALU.mult, ALU.subtract
            )

        for n, t in enumerate(LATE):
            y_late = bank("y%d" % t, [P, S], PACK + n)
            product(y_late[:], everything, w1_dealt, w1_dealt_plane, t, x1_words, x1_plane, True, True)
            keep_y(t, y_late)
        fetch_members(False, LATE[1])
        fetch_members(True, LATE[0])

        for t in range(PACK):
            nc.scalar.activation(size[:, t, :], diff[:, t, :], ACT.Abs, scale=gk_inv[:, t : t + 1])
        for t in range(PACK):
            nc.scalar.activation(log_size[t], size[:, t, :], ACT.Ln, bias=eight)

        larger = tile("larger", [P, PACK, S], F32, tag="key_words")
        st = tile("st", [P, (PACK - 1) * S + WIDE], F32)
        nc.gpsimd.memset(st[:, PACK * S :], 0.0)
        st_at_n2 = tile("st_at_n2", [P, PACK, S], F32)
        for t in EARLY + LATE:
            pairs = y_members[t].rearrange("p (j u) -> p j u", u=2)
            nc.vector.tensor_tensor(larger[:, t, :], pairs[:, :, 0], pairs[:, :, 1], ALU.max)
            nc.vector.tensor_tensor(st[:, t * S : (t + 1) * S], y[t][:, :S], larger[:, t, :], ALU.subtract)
            nc.vector.tensor_copy(st_at_n2[:, t, :], st[:, t * S : t * S + WIDE].indirect(n2_t[:]))

        inverse = tile("inverse", [P, PACK, S], F32, tag="size")
        for t in range(PACK):
            nc.scalar.activation(inverse[:, t, :], wide[t][:].indirect(n4_t[:]), ACT.Exp, scale=-1.0)

        w2_dealt = deal_words("w2_dealt", w2w[:])
        w3_dealt = deal_words("w3_dealt", w3w[:])
        w23_dealt_plane = deal_bytes("w23_dealt_plane", w23_plane[:])

        halves = [slice(HALF * u, HALF * (u + 1)) for u in range(2)]
        h_ps = [[bank("h%d%d" % (u, t), [P, HALF], PACK * u + t) for t in range(PACK)] for u in range(2)]
        z_woven = tile("z_woven", [P, S, PACK], BF16)
        z_words = tile("z_words", [P, S], U32)
        z_plane = tile("z_plane", [P, S], U8)
        unsigned = tile("unsigned", [P, S, PACK], BF16)
        st_tiles = st[:, : PACK * S].rearrange("p (t j) -> p t j", t=PACK)
        nc.vector.tensor_tensor(woven(unsigned[:]), by_tiles(st_tiles), by_tiles(st_at_n2[:]), ALU.max)
        runs = S // SIGN_COLUMNS
        nc.vector.tensor_tensor(
            z_woven[:].rearrange("p (r j) t -> p r (j t)", r=runs),
            unsigned[:].rearrange("p (r j) t -> p r (j t)", r=runs),
            gn_sign[:].rearrange("p j t -> p (j t)").unsqueeze(1).to_broadcast([P, runs, SIGN_COLUMNS * PACK]),
            ALU.mult,
        )
        quantise(z_words[:], z_plane[:], z_woven[:])
        for u in range(2):
            for t in range(PACK):
                product(h_ps[u][t][:], halves[u], w2_dealt, w23_dealt_plane, t, z_words, z_plane, True, False)

        z2_words = tile("z2_words", [P, S], U32)
        z2_plane = tile("z2_plane", [P, S], U8)
        ex = [window("ex_window%d" % t) for t in range(PACK)]
        ex_inv = tile("ex_inv", [P, PACK, HALF], F32)

        for u in range(2):
            z2_woven = tile("z2_woven%d" % u, [P, HALF, PACK], BF16, tag="z_woven")
            nc.vector.tensor_tensor(
                woven(z2_woven[:]), by_tiles(diff[:, :, halves[u]]), by_tiles(inverse[:, :, halves[u]]), ALU.mult
            )
            quantise(z2_words[:, halves[u]], z2_plane[:, halves[u]], z2_woven[:])
            for t in range(PACK):
                product(
                    h_ps[u][t][:], halves[u], w3_dealt, w23_dealt_plane[4:P, :], t, z2_words, z2_plane, False, True
                )
            for t in range(PACK):
                nc.scalar.activation(ex[t][:, halves[u]], h_ps[u][t][:], ACT.Exp)

        out_codes = tile("out_codes", [P, S], U32)
        out_plane = tile("out_plane", [P, S], U8)
        out_rows = out_0.rearrange("(p t) j -> p t j", t=PACK)
        out_words = out_1[0].rearrange("p n t -> p (n t)").bitcast(I32)
        chunks = [slice(CHUNK * c, CHUNK * (c + 1)) for c in range(S // CHUNK)]
        per_half = HALF // CHUNK
        h_low = tile("h_low", [P, PACK, HALF], F32, tag="z_woven")
        for t in range(PACK):
            nc.vector.tensor_copy(h_low[:, t, :], h_ps[0][t][:])
        fetched = [tile("fetched%d" % c, [P, PACK, CHUNK, MEMBERS], F32) for c in range(len(chunks))]
        before_log = {}

        def fetch_ex(on_vector, c, t):
            gather(
                on_vector,
                fetched[c][:, t, :, :].rearrange("p j u -> p (j u)"),
                ex[t],
                n5_t[:, span * c : span * (c + 1)],
            )

        for c in range(per_half):
            before_log[c] = bank("turned%d" % c, [P, PACK, CHUNK], c)
        for t in range(PACK):
            for c in range(per_half):
                fetch_ex(True, c, t)
                terms = [ex[t][:, chunks[c]]] + [fetched[c][:, t, :, u] for u in range(MEMBERS)]
                for n, term in enumerate(terms):
                    nc.tensor.matmul(
                        before_log[c][:, t, :], term, ident[:], is_transpose=True, start=n == 0, stop=n == MEMBERS
                    )

        def add_members(adder, c, lo, hi):
            quads = fetched[c][:, lo:hi, :, :].rearrange("p t j u -> p (t j) u")
            twos = tile("twos%d%d" % (c, lo), [P, (hi - lo) * CHUNK, 2], F32)
            adder.tensor_tensor(twos[:], quads[:, :, 0:2], quads[:, :, 2:4], ALU.add)
            total = tile("total%d%d" % (c, lo), [P, hi - lo, CHUNK], F32)
            adder.tensor_tensor(total[:].rearrange("p t j -> p (t j)"), twos[:, :, 0], twos[:, :, 1], ALU.add)
            adder.tensor_tensor(
                before_log[c][:, lo:hi, :], total[:], ex_inv[:, lo:hi, chunks[c - per_half]], ALU.mult
            )

        third, last = per_half, per_half + 1
        for t in range(PACK):
            fetch_ex(False, third, t)
        for t in range(PACK):
            nc.scalar.activation(ex_inv[:, t, :], h_ps[1][t][:], ACT.Exp, scale=-1.0)
        before_log[third] = tile("ratio%d" % third, [P, PACK, CHUNK], F32)
        add_members(nc.gpsimd, third, 0, PACK // 2)
        add_members(nc.gpsimd, third, PACK // 2, PACK)
        for t in range(PACK):
            fetch_ex(t == PACK - 1, last, t)
        before_log[last] = tile("ratio%d" % last, [P, PACK, CHUNK], F32)
        add_members(nc.gpsimd, last, 0, LAST_ON_GPSIMD)
        add_members(nc.vector, last, LAST_ON_GPSIMD, PACK)

        for c, cols in enumerate(chunks):
            result = tile("result%d" % c, [P, PACK, CHUNK], F32, tag="fetched%d" % (c - 1) if c == third else "")
            rounded = tile("rounded%d" % c, [P, CHUNK, PACK], BF16)
            if c < per_half:
                logs = tile("logs%d" % c, [P, PACK, CHUNK], F32)
                nc.scalar.activation(logs[:], before_log[c][:], ACT.Ln)
                back = bank("back%d" % c, [P, PACK, CHUNK], per_half + c)
                for t in range(PACK):
                    nc.tensor.transpose(back[:, t, :], logs[:, t, :], ident[:])
                nc.vector.tensor_tensor(result[:], back[:], h_low[:, :, cols], ALU.subtract)
                round_once = nc.vector.tensor_copy
            else:
                nc.scalar.activation(result[:], before_log[c][:], ACT.Ln, bias=one)
                round_once = nc.scalar.copy
            nc.sync.dma_start(out_rows[:, :, cols], result[:])
            round_once(woven(rounded[:]), by_tiles(result[:]))
            quantise(out_codes[:, cols], out_plane[:, cols], rounded[:])
            if c % per_half == per_half - 1:
                done = halves[c // per_half]
                nc.sync.dma_start(out_words[:, done], out_codes[:, done].bitcast(I32))
        for q in range(QUADRANTS):
            queue = nc.sync if q < QUADRANTS // 2 else nc.scalar
            queue.dma_start(
                out_2[0, 4 * q : 4 * q + 4, :].bitcast(I32), out_plane[32 * q : 32 * q + 4, :].bitcast(I32)
            )
